import numpy as np, ml_dtypes
CORES = [1,14,19,24,37,42,55,60,65,78,83,88,101,106,119,124]
N = 16
import mx_ref
NC, KT, ROOT = 512, 1, 9
BF = ml_dtypes.bfloat16
def setup_inputs(rng):
    def f(*shape):
        return mx_ref.flush((rng.standard_normal(shape, dtype=np.float32) * np.exp2(rng.integers(-2, 3, shape[:-1] + (1,)))).astype(BF))
    return {"w": f(N, 128, KT * 512), "x": f(N, 128, KT * 4 * NC)}
def setup_inputs_blocks(rng):
    d = setup_inputs(rng)
    for k in ("w", "x"): d[k] = mx_ref.spread(d[k], rng, 4)
    return d
def setup_inputs_wide(rng):
    d = setup_inputs(rng)
    for k in ("w", "x"): d[k] = mx_ref.flush((d[k].astype(np.float32) * np.exp2(rng.integers(-8, 9, (N, 1, 1))).astype(np.float32)).astype(BF))
    return d
def setup_inputs_zeros(rng):
    d = setup_inputs(rng); v = d["x"].reshape(N, 128, -1, 4).copy()
    v[np.broadcast_to((rng.random((N, 1, v.shape[2], 1)) < 0.33), v.shape)] = 0
    d["x"] = v.reshape(d["x"].shape)
    return d
def reference(w, x):
    QW = [mx_ref.quantize(w[ROOT][:, 512 * t:512 * t + 512]) for t in range(KT)]
    y = np.zeros((N, 128, NC), np.float32)
    for r in range(N):
        for t in range(KT):
            p = mx_ref.matmul(QW[t], mx_ref.quantize(x[r][:, 4 * NC * t:4 * NC * t + 4 * NC]))
            y[r] = p if t == 0 else y[r] + p
    return {"y": y}

@@ -1,0 +1,121 @@
+from concourse.bass import DstId, RemoteDMATransfer
+from concourse.mybir import dt, ActivationFunctionType
+
+SCRATCH = {
+    "wb": ("sbuf", [128, 512], "bfloat16"),
+    "xb": ("sbuf", [128, 2048], "bfloat16"),
+    "wq": ("sbuf", [128, 128], "float8_e4m3fn_x4"),
+    "ws": ("sbuf", [128, 128], "uint8"),
+    "xq": ("sbuf", [128, 512], "float8_e4m3fn_x4"),
+    "xs": ("sbuf", [128, 512], "uint8"),
+    "yb": ("sbuf", [128, 512], "float32"),
+    "ps": ("psum", [128, 1024], "float32"),
+}
+SEMAPHORES = ["wl", "xl", "wqd", "xqd", "sarr", "carr", "sent", "mm0", "mm1", "ev0", "ev1", "st"]
+
+EXTRA = 1
+
+
+def _plan(T, topo):
+    cores = list(T.cores)
+    root = cores[T.root]
+    dests = [c for c in cores if c != root]
+    home = [c for c in range(topo.CHIPS * topo.CORES_PER_CHIP)
+            if topo.chip(c) == topo.chip(root) and c not in cores]
+    free = [c for c in home if all(topo.may_write(c, d) for d in dests)]
+    bound = sorted([c for c in home if c not in free], key=lambda c: topo.die(c) != topo.die(root))
+    helpers = free + bound[:EXTRA]
+    senders = [root] + helpers
+    cap = -(-len(dests) // len(senders))
+    load = {s: [] for s in senders}
+    hard = [d for d in dests if not all(topo.may_write(s, d) for s in senders)]
+    for d in hard + [d for d in dests if d not in hard]:
+        ok = [s for s in senders if topo.may_write(s, d) and len(load[s]) < cap]
+        s = min(ok, key=lambda s: (topo.die(s) != topo.die(d), len(load[s]), senders.index(s)))
+        load[s].append(d)
+    return root, helpers, load
+
+
+def _mask(topo, src, dsts):
+    m = topo.mask(src, dsts[0])
+    for d in dsts[1:]:
+        m &= topo.mask(src, d)
+    return m, bin(m).count("1")
+
+
+def _send(g, T, topo, src, dsts, codes):
+    m, n = _mask(topo, src, dsts)
+
+    def view():
+        return T.wq[:].bitcast(dt.uint8) if codes else T.ws[:]
+
+    g.remote_dma_fused(
+        [RemoteDMATransfer(dst_ids=[DstId(rid=topo.addr(d)[0], pnc=topo.addr(d)[1]) for d in dsts],
+                           dma_engine_mask=m, remote_sem=T.sem.carr if codes else T.sem.sarr,
+                           srcs=[view()], dsts=[view() for _ in dsts])],
+        local_sem=T.sem.sent)
+    return n
+
+
+def rank_program(g, core, T, topo):
+    root, helpers, load = _plan(T, topo)
+    rank = T.rank_of(core)
+    if rank is None and core not in helpers:
+        return
+
+    arrive = 0
+    if core in helpers:
+        arrive = _mask(topo, root, helpers)[1]
+    elif core != root:
+        sender = [s for s in load if core in load[s]][0]
+        arrive = _mask(topo, sender, load[sender])[1]
+
+    if core == root:
+        g.sync.dma_start(T.wb[:], T.w[:]).then_inc(T.sem.wl, 16)
+    if rank is not None:
+        g.sync.dma_start(T.xb[:], T.x[:]).then_inc(T.sem.xl, 16)
+    if core == root:
+        g.vector.wait_ge(T.sem.wl, 16)
+        g.vector.quantize_mx(T.wq[:], T.ws[:], T.wb[:]).then_inc(T.sem.wqd, 1)
+    if rank is not None:
+        g.vector.wait_ge(T.sem.xl, 16)
+        g.vector.quantize_mx(T.xq[:], T.xs[:], T.xb[:]).then_inc(T.sem.xqd, 1)
+
+    sent = 0
+    if core == root:
+        g.wait_ge(T.sem.wqd, 1)
+        sent += _send(g, T, topo, core, helpers, False)
+        sent += _send(g, T, topo, core, helpers, True)
+        sent += _send(g, T, topo, core, load[core], False)
+        sent += _send(g, T, topo, core, load[core], True)
+    elif core in helpers:
+        g.wait_ge(T.sem.sarr, arrive)
+        sent += _send(g, T, topo, core, load[core], False)
+        g.wait_ge(T.sem.carr, arrive)
+        sent += _send(g, T, topo, core, load[core], True)
+    if sent:
+        g.wait_ge(T.sem.sent, sent)
+    if rank is None:
+        return
+
+    g.tensor.wait_ge(T.sem.xqd, 1)
+    if core == root:
+        g.tensor.wait_ge(T.sem.wqd, 1)
+    else:
+        g.tensor.wait_ge(T.sem.sarr, arrive)
+        g.tensor.wait_ge(T.sem.carr, arrive)
+    g.tensor.matmul_mx(T.ps[:, 0:256], T.wq[:], T.ws[:], T.xq[:, 0:256], T.xs[:, 0:256],
+                       True, True).then_inc(T.sem.mm0, 1)
+    g.tensor.matmul_mx(T.ps[:, 512:768], T.wq[:], T.ws[:], T.xq[:, 256:512], T.xs[:, 256:512],
+                       True, True).then_inc(T.sem.mm1, 1)
+    g.vector.wait_ge(T.sem.mm0, 1)
+    g.vector.tensor_copy(T.yb[:, 0:256], T.ps[:, 0:256]).then_inc(T.sem.ev0, 1)
+    g.scalar.wait_ge(T.sem.mm1, 1)
+    g.scalar.activation(T.yb[:, 256:512], T.ps[:, 512:768], ActivationFunctionType.Copy).then_inc(T.sem.ev1, 1)
+
+    g.sync.wait_ge(T.sem.ev0, 1)
+    g.sync.wait_ge(T.sem.ev1, 1)
+    if sent:
+        g.sync.wait_ge(T.sem.sent, sent)
+    g.sync.dma_start(T.y[:], T.yb[:]).then_inc(T.sem.st, 16)
+    g.sync.wait_ge(T.sem.st, 16)

@@ -9,11 +9,12 @@ SCRATCH = {
     "xq": ("sbuf", [128, 512], "float8_e4m3fn_x4"),
     "xs": ("sbuf", [128, 512], "uint8"),
     "yb": ("sbuf", [128, 512], "float32"),
-    "ps": ("psum", [128, 1024], "float32"),
+    "ps": ("psum", [128, 2048], "float32"),
 }
-SEMAPHORES = ["wl", "xl", "wqd", "xqd", "sarr", "carr", "sent", "mm0", "mm1", "ev0", "ev1", "st"]
+SEMAPHORES = ["wl", "xl", "wqd", "xqd", "sarr", "carr", "sent", "mm0", "mm1", "mm2", "mm3", "eva", "evb", "st"]
 
-EXTRA = 1
+HELPERS = 6
+SHARE = 2
 
 
 def _plan(T, topo):
@@ -23,29 +24,33 @@ def _plan(T, topo):
     home = [c for c in range(topo.CHIPS * topo.CORES_PER_CHIP)
             if topo.chip(c) == topo.chip(root) and c not in cores]
     free = [c for c in home if all(topo.may_write(c, d) for d in dests)]
-    bound = sorted([c for c in home if c not in free], key=lambda c: topo.die(c) != topo.die(root))
-    helpers = free + bound[:EXTRA]
+    bound = sorted([c for c in home if c not in free], key=lambda c: topo.die(c) == topo.die(root))
+    helpers = (free + bound)[:HELPERS]
+    groups = [helpers[:len(helpers) // 2], helpers[len(helpers) // 2:]]
     senders = [root] + helpers
-    cap = -(-len(dests) // len(senders))
+    cap = {s: SHARE for s in helpers}
+    cap[root] = len(dests) - SHARE * len(helpers)
     load = {s: [] for s in senders}
     hard = [d for d in dests if not all(topo.may_write(s, d) for s in senders)]
     for d in hard + [d for d in dests if d not in hard]:
-        ok = [s for s in senders if topo.may_write(s, d) and len(load[s]) < cap]
+        ok = [s for s in senders if topo.may_write(s, d) and len(load[s]) < cap[s]]
         s = min(ok, key=lambda s: (topo.die(s) != topo.die(d), len(load[s]), senders.index(s)))
         load[s].append(d)
-    return root, helpers, load
+    return root, groups, load
 
 
 def _mask(topo, src, dsts):
     m = topo.mask(src, dsts[0])
     for d in dsts[1:]:
         m &= topo.mask(src, d)
-    return m, bin(m).count("1")
+    return m
 
 
-def _send(g, T, topo, src, dsts, codes):
-    m, n = _mask(topo, src, dsts)
+def _count(m):
+    return bin(m).count("1")
 
+
+def _send(g, T, topo, dsts, codes, m):
     def view():
         return T.wq[:].bitcast(dt.uint8) if codes else T.ws[:]
 
@@ -54,21 +59,27 @@ def _send(g, T, topo, src, dsts, codes):
                            dma_engine_mask=m, remote_sem=T.sem.carr if codes else T.sem.sarr,
                            srcs=[view()], dsts=[view() for _ in dsts])],
         local_sem=T.sem.sent)
-    return n
+    return _count(m)
 
 
 def rank_program(g, core, T, topo):
-    root, helpers, load = _plan(T, topo)
+    root, groups, load = _plan(T, topo)
+    helpers = groups[0] + groups[1]
     rank = T.rank_of(core)
     if rank is None and core not in helpers:
         return
 
-    arrive = 0
+    whole = _mask(topo, root, helpers)
+    away = _mask(topo, root, load[root])
+    halves = [whole & away, whole & ~away]
+
+    s_arr = c_arr = 0
     if core in helpers:
-        arrive = _mask(topo, root, helpers)[1]
+        s_arr = _count(halves[0] if core in groups[0] else halves[1])
+        c_arr = _count(whole)
     elif core != root:
         sender = [s for s in load if core in load[s]][0]
-        arrive = _mask(topo, sender, load[sender])[1]
+        s_arr = c_arr = _count(_mask(topo, sender, load[sender]))
 
     if core == root:
         g.sync.dma_start(T.wb[:], T.w[:]).then_inc(T.sem.wl, 16)
@@ -84,15 +95,17 @@ def rank_program(g, core, T, topo):
     sent = 0
     if core == root:
         g.wait_ge(T.sem.wqd, 1)
-        sent += _send(g, T, topo, core, helpers, False)
-        sent += _send(g, T, topo, core, helpers, True)
-        sent += _send(g, T, topo, core, load[core], False)
-        sent += _send(g, T, topo, core, load[core], True)
+        sent += _send(g, T, topo, groups[0], False, halves[0])
+        sent += _send(g, T, topo, groups[1], False, halves[1])
+        sent += _send(g, T, topo, helpers, True, whole)
+        sent += _send(g, T, topo, load[core], False, away)
+        sent += _send(g, T, topo, load[core], True, away)
     elif core in helpers:
-        g.wait_ge(T.sem.sarr, arrive)
-        sent += _send(g, T, topo, core, load[core], False)
-        g.wait_ge(T.sem.carr, arrive)
-        sent += _send(g, T, topo, core, load[core], True)
+        m = _mask(topo, core, load[core])
+        g.wait_ge(T.sem.sarr, s_arr)
+        sent += _send(g, T, topo, load[core], False, m)
+        g.wait_ge(T.sem.carr, c_arr)
+        sent += _send(g, T, topo, load[core], True, m)
     if sent:
         g.wait_ge(T.sem.sent, sent)
     if rank is None:
@@ -102,20 +115,26 @@ def rank_program(g, core, T, topo):
     if core == root:
         g.tensor.wait_ge(T.sem.wqd, 1)
     else:
-        g.tensor.wait_ge(T.sem.sarr, arrive)
-        g.tensor.wait_ge(T.sem.carr, arrive)
-    g.tensor.matmul_mx(T.ps[:, 0:256], T.wq[:], T.ws[:], T.xq[:, 0:256], T.xs[:, 0:256],
-                       True, True).then_inc(T.sem.mm0, 1)
-    g.tensor.matmul_mx(T.ps[:, 512:768], T.wq[:], T.ws[:], T.xq[:, 256:512], T.xs[:, 256:512],
-                       True, True).then_inc(T.sem.mm1, 1)
-    g.vector.wait_ge(T.sem.mm0, 1)
-    g.vector.tensor_copy(T.yb[:, 0:256], T.ps[:, 0:256]).then_inc(T.sem.ev0, 1)
-    g.scalar.wait_ge(T.sem.mm1, 1)
-    g.scalar.activation(T.yb[:, 256:512], T.ps[:, 512:768], ActivationFunctionType.Copy).then_inc(T.sem.ev1, 1)
+        g.tensor.wait_ge(T.sem.sarr, s_arr)
+        g.tensor.wait_ge(T.sem.carr, c_arr)
+    for q in range(4):
+        g.tensor.matmul_mx(T.ps[:, 512 * q:512 * q + 128], T.wq[:], T.ws[:],
+                           T.xq[:, 128 * q:128 * q + 128], T.xs[:, 128 * q:128 * q + 128],
+                           True, True).then_inc(T.sem["mm%d" % q], 1)
+    for q in range(4):
+        done = T.sem.eva if q < 2 else T.sem.evb
+        out, src = T.yb[:, 128 * q:128 * q + 128], T.ps[:, 512 * q:512 * q + 128]
+        if q % 2 == 0:
+            g.vector.wait_ge(T.sem["mm%d" % q], 1)
+            g.vector.tensor_copy(out, src).then_inc(done, 1)
+        else:
+            g.scalar.wait_ge(T.sem["mm%d" % q], 1)
+            g.scalar.activation(out, src, ActivationFunctionType.Copy).then_inc(done, 1)
 
-    g.sync.wait_ge(T.sem.ev0, 1)
-    g.sync.wait_ge(T.sem.ev1, 1)
+    g.sync.wait_ge(T.sem.eva, 2)
     if sent:
         g.sync.wait_ge(T.sem.sent, sent)
-    g.sync.dma_start(T.y[:], T.yb[:]).then_inc(T.sem.st, 16)
-    g.sync.wait_ge(T.sem.st, 16)
+    g.sync.dma_start(T.y[:, 0:256], T.yb[:, 0:256]).then_inc(T.sem.st, 16)
+    g.sync.wait_ge(T.sem.evb, 2)
+    g.sync.dma_start(T.y[:, 256:512], T.yb[:, 256:512]).then_inc(T.sem.st, 16)
+    g.sync.wait_ge(T.sem.st, 32)

from concourse.bass import DstId, RemoteDMATransfer
from concourse.mybir import dt, ActivationFunctionType

SCRATCH = {
    "wb": ("sbuf", [128, 512], "bfloat16"),
    "xb": ("sbuf", [128, 2048], "bfloat16"),
    "wq": ("sbuf", [128, 128], "float8_e4m3fn_x4"),
    "ws": ("sbuf", [128, 128], "uint8"),
    "xq": ("sbuf", [128, 512], "float8_e4m3fn_x4"),
    "xs": ("sbuf", [128, 512], "uint8"),
    "yb": ("sbuf", [128, 512], "float32"),
    "ps": ("psum", [128, 2048], "float32"),
}
SEMAPHORES = ["wl", "xl", "wqd", "xqd", "sarr", "carr", "sent", "mm0", "mm1", "mm2", "mm3", "eva", "evb", "st"]

HELPERS = 6
SHARE = 2


def _plan(T, topo):
    cores = list(T.cores)
    root = cores[T.root]
    dests = [c for c in cores if c != root]
    home = [c for c in range(topo.CHIPS * topo.CORES_PER_CHIP)
            if topo.chip(c) == topo.chip(root) and c not in cores]
    free = [c for c in home if all(topo.may_write(c, d) for d in dests)]
    bound = sorted([c for c in home if c not in free], key=lambda c: topo.die(c) == topo.die(root))
    helpers = (free + bound)[:HELPERS]
    groups = [helpers[:len(helpers) // 2], helpers[len(helpers) // 2:]]
    senders = [root] + helpers
    cap = {s: SHARE for s in helpers}
    cap[root] = len(dests) - SHARE * len(helpers)
    load = {s: [] for s in senders}
    hard = [d for d in dests if not all(topo.may_write(s, d) for s in senders)]
    for d in hard + [d for d in dests if d not in hard]:
        ok = [s for s in senders if topo.may_write(s, d) and len(load[s]) < cap[s]]
        s = min(ok, key=lambda s: (topo.die(s) != topo.die(d), len(load[s]), senders.index(s)))
        load[s].append(d)
    return root, groups, load


def _mask(topo, src, dsts):
    m = topo.mask(src, dsts[0])
    for d in dsts[1:]:
        m &= topo.mask(src, d)
    return m


def _count(m):
    return bin(m).count("1")


def _send(g, T, topo, dsts, codes, m):
    def view():
        return T.wq[:].bitcast(dt.uint8) if codes else T.ws[:]

    g.remote_dma_fused(
        [RemoteDMATransfer(dst_ids=[DstId(rid=topo.addr(d)[0], pnc=topo.addr(d)[1]) for d in dsts],
                           dma_engine_mask=m, remote_sem=T.sem.carr if codes else T.sem.sarr,
                           srcs=[view()], dsts=[view() for _ in dsts])],
        local_sem=T.sem.sent)
    return _count(m)


def rank_program(g, core, T, topo):
    root, groups, load = _plan(T, topo)
    helpers = groups[0] + groups[1]
    rank = T.rank_of(core)
    if rank is None and core not in helpers:
        return

    whole = _mask(topo, root, helpers)
    away = _mask(topo, root, load[root])
    halves = [whole & away, whole & ~away]

    s_arr = c_arr = 0
    if core in helpers:
        s_arr = _count(halves[0] if core in groups[0] else halves[1])
        c_arr = _count(whole)
    elif core != root:
        sender = [s for s in load if core in load[s]][0]
        s_arr = c_arr = _count(_mask(topo, sender, load[sender]))

    if core == root:
        g.sync.dma_start(T.wb[:], T.w[:]).then_inc(T.sem.wl, 16)
    if rank is not None:
        g.sync.dma_start(T.xb[:], T.x[:]).then_inc(T.sem.xl, 16)
    if core == root:
        g.vector.wait_ge(T.sem.wl, 16)
        g.vector.quantize_mx(T.wq[:], T.ws[:], T.wb[:]).then_inc(T.sem.wqd, 1)
    if rank is not None:
        g.vector.wait_ge(T.sem.xl, 16)
        g.vector.quantize_mx(T.xq[:], T.xs[:], T.xb[:]).then_inc(T.sem.xqd, 1)

    sent = 0
    if core == root:
        g.wait_ge(T.sem.wqd, 1)
        sent += _send(g, T, topo, groups[0], False, halves[0])
        sent += _send(g, T, topo, groups[1], False, halves[1])
        sent += _send(g, T, topo, helpers, True, whole)
        sent += _send(g, T, topo, load[core], False, away)
        sent += _send(g, T, topo, load[core], True, away)
    elif core in helpers:
        m = _mask(topo, core, load[core])
        g.wait_ge(T.sem.sarr, s_arr)
        sent += _send(g, T, topo, load[core], False, m)
        g.wait_ge(T.sem.carr, c_arr)
        sent += _send(g, T, topo, load[core], True, m)
    if sent:
        g.wait_ge(T.sem.sent, sent)
    if rank is None:
        return

    g.tensor.wait_ge(T.sem.xqd, 1)
    if core == root:
        g.tensor.wait_ge(T.sem.wqd, 1)
    else:
        g.tensor.wait_ge(T.sem.sarr, s_arr)
        g.tensor.wait_ge(T.sem.carr, c_arr)
    for q in range(4):
        g.tensor.matmul_mx(T.ps[:, 512 * q:512 * q + 128], T.wq[:], T.ws[:],
                           T.xq[:, 128 * q:128 * q + 128], T.xs[:, 128 * q:128 * q + 128],
                           True, True).then_inc(T.sem["mm%d" % q], 1)
    for q in range(4):
        done = T.sem.eva if q < 2 else T.sem.evb
        out, src = T.yb[:, 128 * q:128 * q + 128], T.ps[:, 512 * q:512 * q + 128]
        if q % 2 == 0:
            g.vector.wait_ge(T.sem["mm%d" % q], 1)
            g.vector.tensor_copy(out, src).then_inc(done, 1)
        else:
            g.scalar.wait_ge(T.sem["mm%d" % q], 1)
            g.scalar.activation(out, src, ActivationFunctionType.Copy).then_inc(done, 1)

    g.sync.wait_ge(T.sem.eva, 2)
    if sent:
        g.sync.wait_ge(T.sem.sent, sent)
    g.sync.dma_start(T.y[:, 0:256], T.yb[:, 0:256]).then_inc(T.sem.st, 16)
    g.sync.wait_ge(T.sem.evb, 2)
    g.sync.dma_start(T.y[:, 256:512], T.yb[:, 256:512]).then_inc(T.sem.st, 16)
    g.sync.wait_ge(T.sem.st, 32)
